import numpy as np
import ml_dtypes


def mxq(x, axis, fmt="e4m3"):
    dtype, down = {"e4m3": (ml_dtypes.float8_e4m3fn, 7), "e5m2": (ml_dtypes.float8_e5m2, 14)}[fmt]
    v = np.moveaxis(np.asarray(x, np.float32).astype(ml_dtypes.bfloat16).astype(np.float64), axis, -1)
    blocks = v.reshape(v.shape[:-1] + (-1, 32))
    amax = np.abs(blocks).max(-1, keepdims=True)
    byte = np.maximum(np.where(amax > 0, np.frexp(amax)[1] - 1 + 127, 0) - down, 1)
    scale = np.exp2(byte - 127.0)
    codes = (blocks / scale).astype(np.float32).astype(dtype).astype(np.float64)
    return np.moveaxis((codes * scale).reshape(v.shape), -1, axis)


WIDE = False


def mx_kscale(k):
    if not WIDE:
        return np.ones(k)
    levels = np.array([10, -10, 5, -5, 0])
    if k % 512:
        return np.exp2(np.random.permutation(np.resize(levels, k // 32))).repeat(32)
    a = np.empty((k // 512, 16))
    for p in range(k // 512):
        a[p, :8] = np.random.permutation(np.resize(levels, 8))
        for g in range(8):
            far = levels[np.abs(levels - a[p, g]) >= 10]
            a[p, g + 8] = far[np.random.randint(len(far))]
    return np.exp2(a.ravel()).repeat(32)


def f64(x):
    return np.asarray(x).astype(np.float64)


def striped(idx):
    return np.tile(idx.reshape(-1, 16).T, (8, 1)).astype(np.uint16)


def unstriped(offs):
    return offs[:16].T.reshape(-1).astype(np.int64)


def gelu(v):
    return 0.5 * v * (1.0 + np.tanh(np.sqrt(2.0 / np.pi) * (v + 0.044715 * v**3)))


K, T, E, C, N = 2048, 512, 6, 256, 128
TOP = 3


def by_expert(wq, xq):
    return np.concatenate([wq[e].T @ xq[:, e * C:(e + 1) * C] for e in range(E)], axis=1)


def setup_inputs():
    n = np.random.standard_normal
    s = mx_kscale(K)[:, None]
    deal = np.repeat(np.arange(E), C).reshape(TOP, T)[:, np.random.permutation(T)]
    deal = np.take_along_axis(deal, np.argsort(np.random.rand(TOP, T), axis=0), axis=0)
    for _ in range(8):
        s_, t_ = np.random.permutation(T).reshape(2, -1); r = np.random.randint(TOP, size=T // 2); x, y = deal[r, s_].copy(), deal[r, t_].copy()
        ok = ~((deal[:, s_] == y).any(0) | (deal[:, t_] == x).any(0)); deal[r[ok], s_[ok]] = y[ok]; deal[r[ok], t_[ok]] = x[ok]
    order = np.lexsort((np.random.rand(TOP * T), deal.reshape(-1)))
    slot_token = order % T; pos = np.empty(TOP * T, np.int64); pos[order] = np.arange(TOP * T); pos = pos.reshape(TOP, T)
    g = np.random.uniform(0.5, 1.5, (TOP, T)); g = g / g.sum(0)
    return {
        "xT": (n((K, T)) * s).astype(np.float32),
        "w": (n((E + 1, K, N)) / np.sqrt(K) / s[None]).astype(np.float32),
        "b": (0.3 * n((N, E + 1))).astype(np.float32),
        "gate": np.stack([np.tile(r, (N, 1)) for r in g]).astype(np.float32),
        "offs": striped(slot_token),
        "pos1": striped(pos[0]),
        "pos2": striped(pos[1]),
        "pos3": striped(pos[2]),
    }


def reference(xT, w, b, gate, offs, pos1, pos2, pos3):
    idx = unstriped(offs)
    wq = mxq(f64(w), 1, "e4m3")
    xs = mxq(f64(xT), 0, "e4m3")
    ys = gelu((wq[E].T @ xs) + f64(b)[:, E:])
    xq = mxq(f64(xT)[:, idx], 0, "e4m3")
    y = by_expert(wq, xq)
    y = gelu(y + np.repeat(f64(b)[:, :E], C, axis=1))
    return ys + sum(f64(gate[r]) * y[:, unstriped(p)] for r, p in enumerate((pos1, pos2, pos3)))

@@ -1,0 +1,189 @@
+from contextlib import ExitStack
+
+import concourse.mybir as mybir
+
+K, T, E, C, N = 2048, 512, 6, 256, 128
+FLOPS = 2 * K * N * (E * C + T)
+
+F32 = mybir.dt.float32
+BF16 = mybir.dt.bfloat16
+U32 = mybir.dt.uint32
+U16 = mybir.dt.uint16
+U8 = mybir.dt.uint8
+FP8X4 = mybir.dt.float8_e4m3fn_x4
+GELU = mybir.ActivationFunctionType.Gelu_apprx_tanh
+MULT = mybir.AluOpType.mult
+ADD = mybir.AluOpType.add
+
+P = 128
+PACK = 4
+K_PASS = P * PACK
+PASSES = K // K_PASS
+CHUNK = 2 * C
+CHUNKS = E * C // CHUNK
+PLANES = 2 * PASSES
+WINDOW = 704
+RING = 4
+
+
+def tile_moe_shr_lin_gelu_kernel(tc, xT, w, b, gate, offs, pos1, pos2, pos3, out):
+    nc = tc.nc
+    with ExitStack() as ctx:
+        keep = ctx.enter_context(tc.tile_pool(name="keep", bufs=1))
+        ring = ctx.enter_context(tc.tile_pool(name="ring", bufs=RING))
+        psum = ctx.enter_context(tc.psum_pool(name="psum", bufs=1))
+
+        offs_sb = keep.tile([P, E * C // 16], U16, name="offs_sb")
+        pos_sb = [keep.tile([P, T // 16], U16, name="pos_sb%d" % r) for r in range(3)]
+        b_sb = keep.tile([P, E + 1], F32, name="b_sb")
+        gate_sb = keep.tile([P, 3, T], F32, name="gate_sb")
+        x_raw = {(g, u): keep.tile([P, 2, T], F32, name="x_raw%d_%d" % (g, u)) for g in range(PASSES) for u in range(2)}
+        w_raw = {}
+        for g in range(PASSES):
+            for c in range(CHUNKS):
+                w_raw[g, c] = keep.tile([P, 2, PACK, N], F32, name="w_raw%d_%d" % (g, c))
+            w_raw[g, CHUNKS] = keep.tile([P, 1, PACK, N], F32, name="w_raw%d_s" % g)
+        pairs = keep.tile([P, 2 * ((PLANES - 1) * T + WINDOW)], BF16, name="pairs", align_bytes=64)
+        y = keep.tile([P, E * C], F32, name="y")
+        ys = keep.tile([P, T], F32, name="ys")
+        warm = keep.tile([P, 8], F32, name="warm")
+        acc = [psum.tile([P, C], F32, name="acc%d" % e) for e in range(E)]
+        acc_s = psum.tile([P, T], F32, name="acc_s")
+
+        def plane_start(g, u):
+            return (2 * (PASSES - 1 - g) + u) * T
+
+        def load_x(g, u):
+            rows = xT[g * K_PASS:(g + 1) * K_PASS, :].rearrange("(p u e) t -> p u e t", u=2, e=2)
+            nc.sync.dma_start(out=x_raw[g, u][:], in_=rows[:, u, :, :])
+
+        def load_w(g, c):
+            e0 = 2 * c
+            e1 = min(e0 + 2, E + 1)
+            rows = w[e0:e1, g * K_PASS:(g + 1) * K_PASS, :].rearrange("e (p j) n -> p e (j n)", j=PACK)
+            nc.sync.dma_start(out=w_raw[g, c][:].rearrange("p e j n -> p e (j n)"), in_=rows)
+
+        load_x(0, 1)
+        nc.sync.dma_start(offs_sb[:], offs)
+        load_w(0, 0)
+        load_x(0, 0)
+        for g in range(PASSES):
+            for c in range(CHUNKS):
+                if (g, c) != (0, 0):
+                    load_w(g, c)
+                if c >= 1 and g + 1 < PASSES:
+                    load_x(g + 1, 2 - c)
+            if g >= 1:
+                load_w(g - 1, CHUNKS)
+        load_w(PASSES - 1, CHUNKS)
+        nc.sync.dma_start(out=b_sb[:], in_=b)
+        for r, pos in enumerate((pos1, pos2, pos3)):
+            nc.sync.dma_start(pos_sb[r][:], pos)
+        nc.sync.dma_start(out=gate_sb[:], in_=gate.rearrange("r n t -> n r t"))
+
+        nc.gpsimd.memset(warm[:], 0.0)
+        nc.scalar.activation(warm[:], warm[:], GELU)
+        nc.gpsimd.memset(pairs[:, 2 * PLANES * T:], 0.0)
+
+        def copy_on(engine, dst, src):
+            if engine == "vector":
+                nc.vector.tensor_copy(dst, src)
+            else:
+                nc.scalar.copy(dst, src)
+
+        def cast_pairs(g, u, engine):
+            s = 2 * plane_start(g, u)
+            dst = pairs[:, s:s + 2 * T].rearrange("p (t e) -> p t e", e=2)
+            copy_on(engine, dst, x_raw[g, u][:].rearrange("p e t -> p t e"))
+
+        def gather(g, c):
+            picked = ring.tile([P, 2, CHUNK], U32, name="picked")
+            cols = offs_sb[:, c * CHUNK // 16:(c + 1) * CHUNK // 16]
+            for u in (1, 0):
+                s = 2 * plane_start(g, u)
+                window = pairs[:, s:s + 2 * WINDOW].bitcast(U32)
+                nc.vector.tensor_copy(picked[:, u, :], window.indirect(cols))
+            return picked[:].rearrange("p u s -> p s u")
+
+        def token_pairs(g):
+            s = 2 * plane_start(g, 0)
+            both = pairs[:, s:s + 4 * T].bitcast(U32).rearrange("p (v t) -> p t v", v=2)
+            return both
+
+        def interleave(src, engine):
+            grouped = ring.tile([P, CHUNK * PACK], BF16, name="grouped", align_bytes=64)
+            dst = grouped[:].bitcast(U32).rearrange("p (s u) -> p s u", u=2)
+            copy_on(engine, dst, src)
+            return grouped
+
+        def cast_w(g, c):
+            ne = w_raw[g, c].shape[1]
+            wb = ring.tile([P, ne * N * PACK], BF16, name="wb", align_bytes=64)
+            for e in range(ne):
+                dst = wb[:, e * N * PACK:(e + 1) * N * PACK].rearrange("p (m i j) -> p m j i", i=4, j=PACK)
+                src = w_raw[g, c][:, e, :, :].rearrange("p j (m i) -> p m j i", i=4)
+                nc.scalar.copy(dst, src)
+            return wb
+
+        def quantize(src, tag):
+            width = src.shape[1] // PACK
+            codes = ring.tile([P, width], U32, name=tag + "_codes", align_bytes=64)
+            scales = ring.tile([P, width], U8, name=tag + "_scales", align_bytes=64)
+            nc.vector.quantize_mx(out=codes[:].bitcast(FP8X4), scales=scales[:], in_=src[:])
+            return codes, scales
+
+        def multiply(dst, g, wq, w_cols, xq, x_cols):
+            nc.tensor.matmul_mx(
+                out=dst, lhsT=wq[0][:, w_cols].bitcast(FP8X4), lhsT_scale=wq[1][:, w_cols],
+                rhs=xq[0][:, x_cols].bitcast(FP8X4), rhs_scale=xq[1][:, x_cols],
+                start=(g == 0), stop=(g == PASSES - 1))
+
+        def routed(g, c):
+            src = gather(g, c)
+            wb = cast_w(g, c)
+            grouped = interleave(src, "scalar")
+            wq = quantize(wb, "w")
+            xq = quantize(grouped, "x")
+            for i in range(2):
+                e = 2 * c + i
+                multiply(acc[e][:], g, wq, slice(i * N, (i + 1) * N), xq, slice(i * C, (i + 1) * C))
+                if g == PASSES - 1:
+                    nc.scalar.activation(y[:, e * C:(e + 1) * C], acc[e][:], GELU, bias=b_sb[:, e:e + 1])
+
+        def shared(g, engine):
+            wb = cast_w(g, CHUNKS)
+            grouped = interleave(token_pairs(g), engine)
+            wq = quantize(wb, "w")
+            xq = quantize(grouped, "x")
+            multiply(acc_s[:], g, wq, slice(0, N), xq, slice(0, T))
+
+        cast_pairs(0, 1, "vector")
+        cast_pairs(0, 0, "scalar")
+        for g in range(PASSES):
+            for c in range(CHUNKS):
+                routed(g, c)
+                if c < 2 and g + 1 < PASSES:
+                    cast_pairs(g + 1, 1 - c, "scalar")
+            if g >= 1:
+                shared(g - 1, "vector" if g == PASSES - 1 else "scalar")
+
+        part = [keep.tile([P, T], F32, name="part%d" % r) for r in range(3)]
+
+        def fetch(r):
+            nc.vector.tensor_tensor(part[r][:], y[:].indirect(pos_sb[r][:]), gate_sb[:, r, :], MULT)
+
+        fetch(0)
+        shared(PASSES - 1, "scalar")
+        nc.scalar.activation(ys[:], acc_s[:], GELU, bias=b_sb[:, E:E + 1])
+        fetch(1)
+        fetch(2)
+        sum01 = keep.tile([P, T], F32, name="sum01")
+        sum2s = keep.tile([P, T], F32, name="sum2s")
+        total = keep.tile([P, T], F32, name="total")
+        halves = [slice(0, T // 2), slice(T // 2, T)]
+        nc.vector.tensor_tensor(sum01[:], part[0][:], part[1][:], ADD)
+        for h in halves:
+            nc.vector.tensor_tensor(sum2s[:, h], part[2][:, h], ys[:, h], ADD)
+        for h in halves:
+            nc.vector.tensor_tensor(total[:, h], sum01[:, h], sum2s[:, h], ADD)
+            nc.sync.dma_start(out=out[:, h], in_=total[:, h])

@@ -12,6 +12,7 @@ U16 = mybir.dt.uint16
 U8 = mybir.dt.uint8
 FP8X4 = mybir.dt.float8_e4m3fn_x4
 GELU = mybir.ActivationFunctionType.Gelu_apprx_tanh
+COPY = mybir.ActivationFunctionType.Copy
 MULT = mybir.AluOpType.mult
 ADD = mybir.AluOpType.add
 
@@ -21,16 +22,26 @@ K_PASS = P * PACK
 PASSES = K // K_PASS
 CHUNK = 2 * C
 CHUNKS = E * C // CHUNK
+LAST = PASSES - 1
 PLANES = 2 * PASSES
-WINDOW = 704
-RING = 4
+PITCH = 704
+REACH = 8
+WCOLS = N * PACK
+SHARED = CHUNKS
+STEPS = PASSES * CHUNKS
+UNIT = 512
+AHEAD = {2: 1, 4: 1, 5: 2, 7: 1, 8: 2}
+SHARED_AT = {5: 0, 8: 1, 11: 2}
+
+LOADS = [("x",0,1),("w",0,0),("x",1,0),("w",0,1),("x",1,1),("w",0,2),("w",1,0),("x",2,0),("w",1,1),("x",2,1),("w",0,3),("w",1,2),("w",2,0),("x",3,0),("w",2,1),("x",3,1),("w",1,3),("w",2,2),("w",3,0),("w",3,1),("w",3,2),("w",2,3),("w",3,3)]
+W_ENGINE = "gpsimd"
 
 
 def tile_moe_shr_lin_gelu_kernel(tc, xT, w, b, gate, offs, pos1, pos2, pos3, out):
     nc = tc.nc
     with ExitStack() as ctx:
         keep = ctx.enter_context(tc.tile_pool(name="keep", bufs=1))
-        ring = ctx.enter_context(tc.tile_pool(name="ring", bufs=RING))
+        ring = ctx.enter_context(tc.tile_pool(name="ring", bufs=4))
         psum = ctx.enter_context(tc.psum_pool(name="psum", bufs=1))
 
         offs_sb = keep.tile([P, E * C // 16], U16, name="offs_sb")
@@ -42,16 +53,32 @@ def tile_moe_shr_lin_gelu_kernel(tc, xT, w, b, gate, offs, pos1, pos2, pos3, out
         for g in range(PASSES):
             for c in range(CHUNKS):
                 w_raw[g, c] = keep.tile([P, 2, PACK, N], F32, name="w_raw%d_%d" % (g, c))
-            w_raw[g, CHUNKS] = keep.tile([P, 1, PACK, N], F32, name="w_raw%d_s" % g)
-        pairs = keep.tile([P, 2 * ((PLANES - 1) * T + WINDOW)], BF16, name="pairs", align_bytes=64)
+            w_raw[g, SHARED] = keep.tile([P, 1, PACK, N], F32, name="w_raw%d_s" % g)
+        pairs = keep.tile([P, 2 * PLANES * PITCH], BF16, name="pairs", align_bytes=64)
+        words = pairs[:].bitcast(U32)
+        arena = keep.tile([P, 5 * (STEPS + 2) * UNIT], BF16, name="arena", align_bytes=64)
+        w16_first = keep.tile([P, 2 * WCOLS], BF16, name="w16_first", align_bytes=64)
+
+        def units(m, a, z):
+            base = 5 * (m + 2) + 1
+            return arena[:, (base + a) * UNIT:(base + z) * UNIT]
+
+        def picked(n):
+            return units(n - 2, -1, 3)
+
+        def grouped(n):
+            return units(n, 0, 4)
+
+        def w16(n):
+            return units(n - 2, 3, 5) if n else w16_first[:]
+
         y = keep.tile([P, E * C], F32, name="y")
         ys = keep.tile([P, T], F32, name="ys")
         warm = keep.tile([P, 8], F32, name="warm")
+        warm16 = keep.tile([P, 8], BF16, name="warm16")
+        warm_out = keep.tile([P, 8], F32, name="warm_out")
         acc = [psum.tile([P, C], F32, name="acc%d" % e) for e in range(E)]
         acc_s = psum.tile([P, T], F32, name="acc_s")
-
-        def plane_start(g, u):
-            return (2 * (PASSES - 1 - g) + u) * T
 
         def load_x(g, u):
             rows = xT[g * K_PASS:(g + 1) * K_PASS, :].rearrange("(p u e) t -> p u e t", u=2, e=2)
@@ -63,127 +90,139 @@ def tile_moe_shr_lin_gelu_kernel(tc, xT, w, b, gate, offs, pos1, pos2, pos3, out
             rows = w[e0:e1, g * K_PASS:(g + 1) * K_PASS, :].rearrange("e (p j) n -> p e (j n)", j=PACK)
             nc.sync.dma_start(out=w_raw[g, c][:].rearrange("p e j n -> p e (j n)"), in_=rows)
 
-        load_x(0, 1)
-        nc.sync.dma_start(offs_sb[:], offs)
-        load_w(0, 0)
         load_x(0, 0)
-        for g in range(PASSES):
-            for c in range(CHUNKS):
-                if (g, c) != (0, 0):
-                    load_w(g, c)
-                if c >= 1 and g + 1 < PASSES:
-                    load_x(g + 1, 2 - c)
-            if g >= 1:
-                load_w(g - 1, CHUNKS)
-        load_w(PASSES - 1, CHUNKS)
+        nc.sync.dma_start(offs_sb[:], offs)
+        for kind, g, i in LOADS:
+            if kind == "x":
+                load_x(g, i)
+            else:
+                load_w(g, i)
         nc.sync.dma_start(out=b_sb[:], in_=b)
         for r, pos in enumerate((pos1, pos2, pos3)):
             nc.sync.dma_start(pos_sb[r][:], pos)
         nc.sync.dma_start(out=gate_sb[:], in_=gate.rearrange("r n t -> n r t"))
 
-        nc.gpsimd.memset(warm[:], 0.0)
-        nc.scalar.activation(warm[:], warm[:], GELU)
-        nc.gpsimd.memset(pairs[:, 2 * PLANES * T:], 0.0)
+        nc.vector.memset(warm[:], 0.0)
+        nc.vector.memset(words.rearrange("p (i m) -> p i m", m=PITCH)[:, :, T:], 0)
+        nc.scalar.activation(warm_out[:], warm[:], GELU)
+        nc.gpsimd.tensor_scalar(warm16[:], warm[:], 1.0, 0.0, MULT, ADD)
 
         def copy_on(engine, dst, src):
             if engine == "vector":
                 nc.vector.tensor_copy(dst, src)
-            else:
+            elif engine == "scalar":
                 nc.scalar.copy(dst, src)
+            else:
+                nc.gpsimd.tensor_scalar(dst, src, 1.0, 0.0, MULT, ADD)
 
         def cast_pairs(g, u, engine):
-            s = 2 * plane_start(g, u)
+            s = 2 * (2 * g + u) * PITCH
             dst = pairs[:, s:s + 2 * T].rearrange("p (t e) -> p t e", e=2)
             copy_on(engine, dst, x_raw[g, u][:].rearrange("p e t -> p t e"))
 
-        def gather(g, c):
-            picked = ring.tile([P, 2, CHUNK], U32, name="picked")
+        def gather(n, u, ahead):
+            g, c = divmod(n, CHUNKS)
+            s = (2 * g + u) * PITCH
+            width = ahead * PITCH + REACH if ahead else PITCH
             cols = offs_sb[:, c * CHUNK // 16:(c + 1) * CHUNK // 16]
-            for u in (1, 0):
-                s = 2 * plane_start(g, u)
-                window = pairs[:, s:s + 2 * WINDOW].bitcast(U32)
-                nc.vector.tensor_copy(picked[:, u, :], window.indirect(cols))
-            return picked[:].rearrange("p u s -> p s u")
+            nc.vector.tensor_copy(picked(n).bitcast(U32)[:, u * CHUNK:(u + 1) * CHUNK], words[:, s:s + width].indirect(cols))
 
-        def token_pairs(g):
-            s = 2 * plane_start(g, 0)
-            both = pairs[:, s:s + 4 * T].bitcast(U32).rearrange("p (v t) -> p t v", v=2)
-            return both
+        def interleave(dst, src, engine):
+            copy_on(engine, dst.bitcast(U32).rearrange("p (s u) -> p s u", u=2), src)
 
-        def interleave(src, engine):
-            grouped = ring.tile([P, CHUNK * PACK], BF16, name="grouped", align_bytes=64)
-            dst = grouped[:].bitcast(U32).rearrange("p (s u) -> p s u", u=2)
-            copy_on(engine, dst, src)
-            return grouped
+        def slot_tokens(n):
+            interleave(grouped(n), picked(n).bitcast(U32).rearrange("p (u s) -> p s u", u=2), "scalar")
 
-        def cast_w(g, c):
-            ne = w_raw[g, c].shape[1]
-            wb = ring.tile([P, ne * N * PACK], BF16, name="wb", align_bytes=64)
-            for e in range(ne):
-                dst = wb[:, e * N * PACK:(e + 1) * N * PACK].rearrange("p (m i j) -> p m j i", i=4, j=PACK)
-                src = w_raw[g, c][:, e, :, :].rearrange("p j (m i) -> p m j i", i=4)
-                nc.scalar.copy(dst, src)
-            return wb
+        def shared_tokens(g, dst, engine):
+            src = words[:, 2 * g * PITCH:(2 * g + 2) * PITCH].rearrange("p (u m) -> p m u", u=2)[:, :T, :]
+            interleave(dst, src, engine)
+
+        def cast_w(key, dst, engine):
+            if engine == "gpsimd":
+                copy_on(engine, dst.rearrange("p (e n j) -> p e n j", n=N, j=PACK), w_raw[key][:].rearrange("p e j n -> p e n j"))
+            else:
+                for e in range(w_raw[key].shape[1]):
+                    cols = dst[:, e * WCOLS:(e + 1) * WCOLS]
+                    copy_on(engine, cols.rearrange("p (m i j) -> p m j i", i=4, j=PACK),
+                            w_raw[key][:, e, :, :].rearrange("p j (m i) -> p m j i", i=4))
 
         def quantize(src, tag):
             width = src.shape[1] // PACK
             codes = ring.tile([P, width], U32, name=tag + "_codes", align_bytes=64)
             scales = ring.tile([P, width], U8, name=tag + "_scales", align_bytes=64)
-            nc.vector.quantize_mx(out=codes[:].bitcast(FP8X4), scales=scales[:], in_=src[:])
+            nc.vector.quantize_mx(out=codes[:].bitcast(FP8X4), scales=scales[:], in_=src)
             return codes, scales
 
-        def multiply(dst, g, wq, w_cols, xq, x_cols):
-            nc.tensor.matmul_mx(
-                out=dst, lhsT=wq[0][:, w_cols].bitcast(FP8X4), lhsT_scale=wq[1][:, w_cols],
-                rhs=xq[0][:, x_cols].bitcast(FP8X4), rhs_scale=xq[1][:, x_cols],
-                start=(g == 0), stop=(g == PASSES - 1))
+        wq = {}
 
-        def routed(g, c):
-            src = gather(g, c)
-            wb = cast_w(g, c)
-            grouped = interleave(src, "scalar")
-            wq = quantize(wb, "w")
-            xq = quantize(grouped, "x")
+        def multiply(dst, g, wcodes, w0, xcodes, x_cols):
+            w_cols = slice(w0, w0 + N)
+            nc.tensor.matmul_mx(
+                out=dst, lhsT=wcodes[0][:, w_cols].bitcast(FP8X4), lhsT_scale=wcodes[1][:, w_cols],
+                rhs=xcodes[0][:, x_cols].bitcast(FP8X4), rhs_scale=xcodes[1][:, x_cols],
+                start=(g == 0), stop=(g == LAST))
+
+        def routed_tokens(n):
+            g, c = divmod(n, CHUNKS)
             for i in range(2):
                 e = 2 * c + i
-                multiply(acc[e][:], g, wq, slice(i * N, (i + 1) * N), xq, slice(i * C, (i + 1) * C))
-                if g == PASSES - 1:
+                xq = quantize(grouped(n)[:, i * C * PACK:(i + 1) * C * PACK], "x")
+                multiply(acc[e][:], g, wq[n], i * N, xq, slice(0, C))
+                if g == LAST:
                     nc.scalar.activation(y[:, e * C:(e + 1) * C], acc[e][:], GELU, bias=b_sb[:, e:e + 1])
 
-        def shared(g, engine):
-            wb = cast_w(g, CHUNKS)
-            grouped = interleave(token_pairs(g), engine)
-            wq = quantize(wb, "w")
-            xq = quantize(grouped, "x")
-            multiply(acc_s[:], g, wq, slice(0, N), xq, slice(0, T))
+        def routed_weights(n):
+            wq[n] = quantize(w16(n), "w")
 
-        cast_pairs(0, 1, "vector")
-        cast_pairs(0, 0, "scalar")
-        for g in range(PASSES):
-            for c in range(CHUNKS):
-                routed(g, c)
-                if c < 2 and g + 1 < PASSES:
-                    cast_pairs(g + 1, 1 - c, "scalar")
-            if g >= 1:
-                shared(g - 1, "vector" if g == PASSES - 1 else "scalar")
+        def shared_pass(g, tokens, weights):
+            ws = quantize(weights, "ws")
+            xs = quantize(tokens, "xs")
+            multiply(acc_s[:], g, ws, 0, xs, slice(0, T))
+
+        cast_pairs(0, 0, "vector")
+        cast_pairs(0, 1, "scalar")
+        cast_w((0, 0), w16(0), W_ENGINE)
+        cast_w((0, 1), w16(1), W_ENGINE)
+        gather(0, 0, 0)
+        gather(1, 0, 0)
+        gather(0, 1, 0)
+        cast_pairs(1, 0, "scalar")
+        slot_tokens(0)
+        gather(1, 1, 0)
+        cast_pairs(1, 1, "scalar")
+        slot_tokens(1)
+        routed_weights(0)
+        routed_weights(1)
+        routed_tokens(0)
+        for n in range(2, STEPS):
+            g, c = divmod(n, CHUNKS)
+            cast_w((g, c), w16(n), W_ENGINE)
+            if 0 < g < LAST and c < 2:
+                cast_pairs(g + 1, c, "scalar")
+            if n in SHARED_AT:
+                cast_w((SHARED_AT[n], SHARED), units(n - 4, 3, 4), "scalar")
+                shared_tokens(SHARED_AT[n], picked(n - 2), "scalar")
+            gather(n, 0, 0)
+            gather(n, 1, AHEAD.get(n, 0))
+            slot_tokens(n)
+            if n in SHARED_AT:
+                shared_pass(SHARED_AT[n], picked(n - 2), units(n - 4, 3, 4))
+            routed_weights(n)
+            routed_tokens(n - 1)
+        last = STEPS - 1
+        cast_w((LAST, SHARED), units(last - 2, 3, 4), "scalar")
+        routed_tokens(last)
+        shared_tokens(LAST, units(last, -2, 2), "vector")
+        shared_pass(LAST, units(last, -2, 2), units(last - 2, 3, 4))
+        nc.scalar.activation(ys[:], acc_s[:], GELU, bias=b_sb[:, E:E + 1])
 
         part = [keep.tile([P, T], F32, name="part%d" % r) for r in range(3)]
-
-        def fetch(r):
+        for r in range(3):
             nc.vector.tensor_tensor(part[r][:], y[:].indirect(pos_sb[r][:]), gate_sb[:, r, :], MULT)
-
-        fetch(0)
-        shared(PASSES - 1, "scalar")
-        nc.scalar.activation(ys[:], acc_s[:], GELU, bias=b_sb[:, E:E + 1])
-        fetch(1)
-        fetch(2)
-        sum01 = keep.tile([P, T], F32, name="sum01")
-        sum2s = keep.tile([P, T], F32, name="sum2s")
-        total = keep.tile([P, T], F32, name="total")
         halves = [slice(0, T // 2), slice(T // 2, T)]
-        nc.vector.tensor_tensor(sum01[:], part[0][:], part[1][:], ADD)
+        nc.vector.tensor_tensor(part[0][:], part[0][:], part[1][:], ADD)
         for h in halves:
-            nc.vector.tensor_tensor(sum2s[:, h], part[2][:, h], ys[:, h], ADD)
+            nc.vector.tensor_tensor(part[2][:, h], part[2][:, h], ys[:, h], ADD)
         for h in halves:
-            nc.vector.tensor_tensor(total[:, h], sum01[:, h], sum2s[:, h], ADD)
-            nc.sync.dma_start(out=out[:, h], in_=total[:, h])
+            nc.vector.tensor_tensor(part[1][:, h], part[0][:, h], part[2][:, h], ADD)
+            nc.sync.dma_start(out=out[:, h], in_=part[1][:, h])

@@ -24,17 +24,17 @@ CHUNK = 2 * C
 CHUNKS = E * C // CHUNK
 LAST = PASSES - 1
 PLANES = 2 * PASSES
-PITCH = 704
-REACH = 8
+WINDOW = 2048
+SLOTS = E * C
+PLANE_AT = {(3, 0): 0, (2, 0): 1, (3, 1): 2, (1, 0): 3, (2, 1): 4, (0, 0): 5, (1, 1): 6, (0, 1): 7}
 WCOLS = N * PACK
 SHARED = CHUNKS
-STEPS = PASSES * CHUNKS
 UNIT = 512
-AHEAD = {2: 1, 4: 1, 5: 2, 7: 1, 8: 2}
-SHARED_AT = {5: 0, 8: 1, 11: 2}
+LODGED = {("w", 0, 1): 24, ("w", 0, 0): 28, ("x", 2, 1): 32, ("x", 2, 0): 36, ("x", 1, 0): 40, ("x", 1, 1): 44,
+          ("x", 3, 0): 48, ("w", 1, 0): 52, ("w", 1, 1): 56, ("w", 3, 0): 60, ("w", 3, 1): 64, ("w", 3, 2): 68}
 
-LOADS = [("x",0,1),("w",0,0),("x",1,0),("w",0,1),("x",1,1),("w",0,2),("w",1,0),("x",2,0),("w",1,1),("x",2,1),("w",0,3),("w",1,2),("w",2,0),("x",3,0),("w",2,1),("x",3,1),("w",1,3),("w",2,2),("w",3,0),("w",3,1),("w",3,2),("w",2,3),("w",3,3)]
-W_ENGINE = "gpsimd"
+LOADS = [("x",0,0),("x",1,1),("x",1,0),("x",2,1),("w",0,0),("w",0,1),("w",0,2),("w",0,3),("x",2,0),("x",3,1),("w",1,0),("w",1,1),("w",1,2),("w",1,3),("x",3,0),("w",2,0),("w",2,1),("w",2,2),("w",3,0),("w",3,1),("w",3,2),("w",2,3),("w",3,3)]
+W_ENGINE = {}
 
 
 def tile_moe_shr_lin_gelu_kernel(tc, xT, w, b, gate, offs, pos1, pos2, pos3, out):
@@ -48,34 +48,34 @@ def tile_moe_shr_lin_gelu_kernel(tc, xT, w, b, gate, offs, pos1, pos2, pos3, out
         pos_sb = [keep.tile([P, T // 16], U16, name="pos_sb%d" % r) for r in range(3)]
         b_sb = keep.tile([P, E + 1], F32, name="b_sb")
         gate_sb = keep.tile([P, 3, T], F32, name="gate_sb")
-        x_raw = {(g, u): keep.tile([P, 2, T], F32, name="x_raw%d_%d" % (g, u)) for g in range(PASSES) for u in range(2)}
+        pairs = keep.tile([P, 2 * ((PLANES - 1) * T + WINDOW)], BF16, name="pairs", align_bytes=64)
+        words = pairs[:].bitcast(U32)
+        arena = keep.tile([P, 72 * UNIT], BF16, name="arena", align_bytes=64)
+        w16 = [keep.tile([P, E * WCOLS], BF16, name="w16_%d" % g, align_bytes=64) for g in range(PASSES)]
+        picked_at = [0, 12, 24, 36]
+        grouped_at = [24, 36, 48, 60]
+
+        def units(a, count):
+            return arena[:, a * UNIT:(a + count) * UNIT]
+
+        x_raw = {}
         w_raw = {}
         for g in range(PASSES):
+            for u in range(2):
+                if ("x", g, u) in LODGED:
+                    x_raw[g, u] = units(LODGED["x", g, u], 4).bitcast(F32).rearrange("p (e t) -> p e t", e=2)
+                else:
+                    x_raw[g, u] = keep.tile([P, 2, T], F32, name="x_raw%d_%d" % (g, u))[:]
             for c in range(CHUNKS):
-                w_raw[g, c] = keep.tile([P, 2, PACK, N], F32, name="w_raw%d_%d" % (g, c))
-            w_raw[g, SHARED] = keep.tile([P, 1, PACK, N], F32, name="w_raw%d_s" % g)
-        pairs = keep.tile([P, 2 * PLANES * PITCH], BF16, name="pairs", align_bytes=64)
-        words = pairs[:].bitcast(U32)
-        arena = keep.tile([P, 5 * (STEPS + 2) * UNIT], BF16, name="arena", align_bytes=64)
-        w16_first = keep.tile([P, 2 * WCOLS], BF16, name="w16_first", align_bytes=64)
-
-        def units(m, a, z):
-            base = 5 * (m + 2) + 1
-            return arena[:, (base + a) * UNIT:(base + z) * UNIT]
-
-        def picked(n):
-            return units(n - 2, -1, 3)
-
-        def grouped(n):
-            return units(n, 0, 4)
-
-        def w16(n):
-            return units(n - 2, 3, 5) if n else w16_first[:]
+                if ("w", g, c) in LODGED:
+                    w_raw[g, c] = units(LODGED["w", g, c], 4).bitcast(F32).rearrange("p (e j n) -> p e j n", e=2, j=PACK)
+                else:
+                    w_raw[g, c] = keep.tile([P, 2, PACK, N], F32, name="w_raw%d_%d" % (g, c))[:]
+            w_raw[g, SHARED] = keep.tile([P, 1, PACK, N], F32, name="w_raw%d_s" % g)[:]
 
         y = keep.tile([P, E * C], F32, name="y")
         ys = keep.tile([P, T], F32, name="ys")
         warm = keep.tile([P, 8], F32, name="warm")
-        warm16 = keep.tile([P, 8], BF16, name="warm16")
         warm_out = keep.tile([P, 8], F32, name="warm_out")
         acc = [psum.tile([P, C], F32, name="acc%d" % e) for e in range(E)]
         acc_s = psum.tile([P, T], F32, name="acc_s")
@@ -90,7 +90,7 @@ def tile_moe_shr_lin_gelu_kernel(tc, xT, w, b, gate, offs, pos1, pos2, pos3, out
             rows = w[e0:e1, g * K_PASS:(g + 1) * K_PASS, :].rearrange("e (p j) n -> p e (j n)", j=PACK)
             nc.sync.dma_start(out=w_raw[g, c][:].rearrange("p e j n -> p e (j n)"), in_=rows)
 
-        load_x(0, 0)
+        load_x(0, 1)
         nc.sync.dma_start(offs_sb[:], offs)
         for kind, g, i in LOADS:
             if kind == "x":
@@ -103,9 +103,8 @@ def tile_moe_shr_lin_gelu_kernel(tc, xT, w, b, gate, offs, pos1, pos2, pos3, out
         nc.sync.dma_start(out=gate_sb[:], in_=gate.rearrange("r n t -> n r t"))
 
         nc.vector.memset(warm[:], 0.0)
-        nc.vector.memset(words.rearrange("p (i m) -> p i m", m=PITCH)[:, :, T:], 0)
+        nc.vector.memset(words[:, PLANES * T:], 0)
         nc.scalar.activation(warm_out[:], warm[:], GELU)
-        nc.gpsimd.tensor_scalar(warm16[:], warm[:], 1.0, 0.0, MULT, ADD)
 
         def copy_on(engine, dst, src):
             if engine == "vector":
@@ -116,26 +115,30 @@ def tile_moe_shr_lin_gelu_kernel(tc, xT, w, b, gate, offs, pos1, pos2, pos3, out
                 nc.gpsimd.tensor_scalar(dst, src, 1.0, 0.0, MULT, ADD)
 
         def cast_pairs(g, u, engine):
-            s = 2 * (2 * g + u) * PITCH
+            s = 2 * PLANE_AT[g, u] * T
             dst = pairs[:, s:s + 2 * T].rearrange("p (t e) -> p t e", e=2)
             copy_on(engine, dst, x_raw[g, u][:].rearrange("p e t -> p t e"))
 
-        def gather(n, u, ahead):
-            g, c = divmod(n, CHUNKS)
-            s = (2 * g + u) * PITCH
-            width = ahead * PITCH + REACH if ahead else PITCH
-            cols = offs_sb[:, c * CHUNK // 16:(c + 1) * CHUNK // 16]
-            nc.vector.tensor_copy(picked(n).bitcast(U32)[:, u * CHUNK:(u + 1) * CHUNK], words[:, s:s + width].indirect(cols))
+        def gather(g, u):
+            s = PLANE_AT[g, u] * T
+            picked = units(picked_at[g], 12).bitcast(U32)
+            nc.vector.tensor_copy(picked[:, u * SLOTS:(u + 1) * SLOTS], words[:, s:s + WINDOW].indirect(offs_sb[:]))
 
         def interleave(dst, src, engine):
             copy_on(engine, dst.bitcast(U32).rearrange("p (s u) -> p s u", u=2), src)
 
-        def slot_tokens(n):
-            interleave(grouped(n), picked(n).bitcast(U32).rearrange("p (u s) -> p s u", u=2), "scalar")
+        def slot_tokens(g):
+            picked = units(picked_at[g], 12).bitcast(U32).rearrange("p (u s) -> p s u", u=2)
+            if g < LAST:
+                interleave(units(grouped_at[g], 12), picked, "scalar")
+            else:
+                for c in range(CHUNKS):
+                    interleave(units(grouped_at[g] + 4 * c, 4), picked[:, c * CHUNK:(c + 1) * CHUNK, :], "scalar")
 
         def shared_tokens(g, dst, engine):
-            src = words[:, 2 * g * PITCH:(2 * g + 2) * PITCH].rearrange("p (u m) -> p m u", u=2)[:, :T, :]
-            interleave(dst, src, engine)
+            lo, hi = PLANE_AT[g, 0], PLANE_AT[g, 1]
+            planes = words[:, :PLANES * T].rearrange("p (i t) -> p t i", t=T)
+            interleave(dst, planes[:, :, lo:hi + 1:hi - lo], engine)
 
         def cast_w(key, dst, engine):
             if engine == "gpsimd":
@@ -146,6 +149,13 @@ def tile_moe_shr_lin_gelu_kernel(tc, xT, w, b, gate, offs, pos1, pos2, pos3, out
                     copy_on(engine, cols.rearrange("p (m i j) -> p m j i", i=4, j=PACK),
                             w_raw[key][:, e, :, :].rearrange("p j (m i) -> p m j i", i=4))
 
+        def cast_routed(g, c):
+            cast_w((g, c), w16[g][:, 2 * c * WCOLS:2 * (c + 1) * WCOLS], W_ENGINE.get((g, c), "scalar"))
+
+        def cast_shared(g, at):
+            cast_w((g, SHARED), units(at + 4, 1), "scalar")
+            shared_tokens(g, units(at, 4), "scalar")
+
         def quantize(src, tag):
             width = src.shape[1] // PACK
             codes = ring.tile([P, width], U32, name=tag + "_codes", align_bytes=64)
@@ -155,70 +165,85 @@ def tile_moe_shr_lin_gelu_kernel(tc, xT, w, b, gate, offs, pos1, pos2, pos3, out
 
         wq = {}
 
-        def multiply(dst, g, wcodes, w0, xcodes, x_cols):
+        def multiply(dst, place, wcodes, w0, xcodes, x_cols):
             w_cols = slice(w0, w0 + N)
             nc.tensor.matmul_mx(
                 out=dst, lhsT=wcodes[0][:, w_cols].bitcast(FP8X4), lhsT_scale=wcodes[1][:, w_cols],
                 rhs=xcodes[0][:, x_cols].bitcast(FP8X4), rhs_scale=xcodes[1][:, x_cols],
-                start=(g == 0), stop=(g == LAST))
+                start=(place == 0), stop=(place == LAST))
 
-        def routed_tokens(n):
-            g, c = divmod(n, CHUNKS)
-            for i in range(2):
-                e = 2 * c + i
-                xq = quantize(grouped(n)[:, i * C * PACK:(i + 1) * C * PACK], "x")
-                multiply(acc[e][:], g, wq[n], i * N, xq, slice(0, C))
-                if g == LAST:
-                    nc.scalar.activation(y[:, e * C:(e + 1) * C], acc[e][:], GELU, bias=b_sb[:, e:e + 1])
+        def routed_tokens(g):
+            for c in (range(CHUNKS) if g == LAST else reversed(range(CHUNKS))):
+                xq = quantize(units(grouped_at[g] + 4 * c, 4), "x")
+                for i in range(2):
+                    e = 2 * c + i
+                    codes, first = (wq[g][0], e) if c < 2 else (wq[g][1], i)
+                    multiply(acc[e][:], g, codes, first * N, xq, slice(i * C, (i + 1) * C))
+                    if g == LAST:
+                        nc.scalar.activation(y[:, e * C:(e + 1) * C], acc[e][:], GELU, bias=b_sb[:, e:e + 1])
 
-        def routed_weights(n):
-            wq[n] = quantize(w16(n), "w")
+        def routed_weights(g):
+            wq[g] = (quantize(w16[g][:, :4 * WCOLS], "w"), quantize(w16[g][:, 4 * WCOLS:], "wr"))
 
-        def shared_pass(g, tokens, weights):
+        def shared_pass(place, tokens, weights):
             ws = quantize(weights, "ws")
             xs = quantize(tokens, "xs")
-            multiply(acc_s[:], g, ws, 0, xs, slice(0, T))
-
-        cast_pairs(0, 0, "vector")
-        cast_pairs(0, 1, "scalar")
-        cast_w((0, 0), w16(0), W_ENGINE)
-        cast_w((0, 1), w16(1), W_ENGINE)
-        gather(0, 0, 0)
-        gather(1, 0, 0)
-        gather(0, 1, 0)
-        cast_pairs(1, 0, "scalar")
-        slot_tokens(0)
-        gather(1, 1, 0)
-        cast_pairs(1, 1, "scalar")
-        slot_tokens(1)
-        routed_weights(0)
-        routed_weights(1)
-        routed_tokens(0)
-        for n in range(2, STEPS):
-            g, c = divmod(n, CHUNKS)
-            cast_w((g, c), w16(n), W_ENGINE)
-            if 0 < g < LAST and c < 2:
-                cast_pairs(g + 1, c, "scalar")
-            if n in SHARED_AT:
-                cast_w((SHARED_AT[n], SHARED), units(n - 4, 3, 4), "scalar")
-                shared_tokens(SHARED_AT[n], picked(n - 2), "scalar")
-            gather(n, 0, 0)
-            gather(n, 1, AHEAD.get(n, 0))
-            slot_tokens(n)
-            if n in SHARED_AT:
-                shared_pass(SHARED_AT[n], picked(n - 2), units(n - 4, 3, 4))
-            routed_weights(n)
-            routed_tokens(n - 1)
-        last = STEPS - 1
-        cast_w((LAST, SHARED), units(last - 2, 3, 4), "scalar")
-        routed_tokens(last)
-        shared_tokens(LAST, units(last, -2, 2), "vector")
-        shared_pass(LAST, units(last, -2, 2), units(last - 2, 3, 4))
-        nc.scalar.activation(ys[:], acc_s[:], GELU, bias=b_sb[:, E:E + 1])
+            multiply(acc_s[:], place, ws, 0, xs, slice(0, T))
 
         part = [keep.tile([P, T], F32, name="part%d" % r) for r in range(3)]
-        for r in range(3):
+
+        def fetch(r):
             nc.vector.tensor_tensor(part[r][:], y[:].indirect(pos_sb[r][:]), gate_sb[:, r, :], MULT)
+
+        def both_gathers(g):
+            gather(g, 1)
+            gather(g, 0)
+
+        def batch(g):
+            routed_weights(g)
+            shared_pass(g, units(picked_at[g], 4), units(picked_at[g] + 4, 1))
+            routed_tokens(g)
+
+        cast_pairs(0, 1, "vector")
+        for g, u in ((0, 0), (1, 1), (1, 0), (2, 1)):
+            cast_pairs(g, u, "scalar")
+        cast_routed(0, 0)
+        cast_routed(0, 1)
+        both_gathers(0)
+        slot_tokens(0)
+        cast_routed(0, 2)
+        cast_shared(0, picked_at[0])
+        cast_pairs(2, 0, "scalar")
+        both_gathers(1)
+        slot_tokens(1)
+        batch(0)
+        cast_pairs(3, 1, "scalar")
+        for c in range(CHUNKS):
+            cast_routed(1, c)
+        cast_shared(1, picked_at[1])
+        cast_pairs(3, 0, "scalar")
+        both_gathers(2)
+        batch(1)
+        slot_tokens(2)
+        for g in (2, 3):
+            for c in range(CHUNKS):
+                cast_routed(g, c)
+        weights2 = units(picked_at[2] + 5, 1)
+        cast_w((2, SHARED), weights2, "scalar")
+        cast_shared(3, picked_at[2])
+        both_gathers(3)
+        routed_weights(2)
+        routed_tokens(2)
+        slot_tokens(3)
+        routed_weights(3)
+        shared_pass(2, units(picked_at[2], 4), units(picked_at[2] + 4, 1))
+        routed_tokens(3)
+        tokens2 = units(grouped_at[LAST] + 8, 4)
+        shared_tokens(2, tokens2, "vector")
+        shared_pass(3, tokens2, weights2)
+        nc.scalar.activation(ys[:], acc_s[:], GELU, bias=b_sb[:, E:E + 1])
+        for r in range(3):
+            fetch(r)
         halves = [slice(0, T // 2), slice(T // 2, T)]
         nc.vector.tensor_tensor(part[0][:], part[0][:], part[1][:], ADD)
         for h in halves:

@@ -20,234 +20,256 @@ P = 128
 PACK = 4
 K_PASS = P * PACK
 PASSES = K // K_PASS
-CHUNK = 2 * C
-CHUNKS = E * C // CHUNK
 LAST = PASSES - 1
-PLANES = 2 * PASSES
-WINDOW = 2048
+TOP = 3
 SLOTS = E * C
-PLANE_AT = {(3, 0): 0, (2, 0): 1, (3, 1): 2, (1, 0): 3, (2, 1): 4, (0, 0): 5, (1, 1): 6, (0, 1): 7}
-WCOLS = N * PACK
+PER_COLUMN = 16
+CHUNK = 2 * C
+CHUNKS = SLOTS // CHUNK
 SHARED = CHUNKS
-UNIT = 512
-LODGED = {("w", 0, 1): 24, ("w", 0, 0): 28, ("x", 2, 1): 32, ("x", 2, 0): 36, ("x", 1, 0): 40, ("x", 1, 1): 44,
-          ("x", 3, 0): 48, ("w", 1, 0): 52, ("w", 1, 1): 56, ("w", 3, 0): 60, ("w", 3, 1): 64, ("w", 3, 2): 68}
+W_COLS = N * PACK
 
-LOADS = [("x",0,0),("x",1,1),("x",1,0),("x",2,1),("w",0,0),("w",0,1),("w",0,2),("w",0,3),("x",2,0),("x",3,1),("w",1,0),("w",1,1),("w",1,2),("w",1,3),("x",3,0),("w",2,0),("w",2,1),("w",2,2),("w",3,0),("w",3,1),("w",3,2),("w",2,3),("w",3,3)]
-W_ENGINE = {}
+WINDOW = 4 * T
+PLANES = 2 * PASSES
+PLANE_AT = {(3, 0): 0, (2, 0): 1, (3, 1): 2, (1, 0): 3, (2, 1): 4, (0, 0): 5, (1, 1): 6, (0, 1): 7}
+EDGE = 16
+
+UNIT = 512
+HALF_UNITS = 6
+PASS_UNITS = 12
+CHUNK_UNITS = 4
+PICKED_AT = [PASS_UNITS * g for g in range(PASSES)]
+GROUPED_AT = [PASS_UNITS * PASSES] + PICKED_AT[:LAST]
+EARLY_TOKENS_AT = [60, 65]
+LATE_WEIGHTS_AT = 70
+ARENA_UNITS = 74
+
+LODGED_X = {(3, 1): GROUPED_AT[0], (1, 1): PICKED_AT[2], (1, 0): PICKED_AT[2] + 4, (2, 1): PICKED_AT[2] + 8,
+            (2, 0): LATE_WEIGHTS_AT}
+LODGED_W = {(0, 0): EARLY_TOKENS_AT[1] - 2}
+W_IN_X_TILE = {(LAST, 0): (0, 1), (LAST, 1): (0, 0), (LAST, 2): (LAST, 0)}
+
+SCALAR_EXPERTS = 4
+GPSIMD_PLANES = [(1, 0), (2, 1), (2, 0), (3, 1)]
+GPSIMD_PASSES = 2
 
 
 def tile_moe_shr_lin_gelu_kernel(tc, xT, w, b, gate, offs, pos1, pos2, pos3, out):
     nc = tc.nc
     with ExitStack() as ctx:
         keep = ctx.enter_context(tc.tile_pool(name="keep", bufs=1))
-        ring = ctx.enter_context(tc.tile_pool(name="ring", bufs=4))
+        ring = ctx.enter_context(tc.tile_pool(name="ring", bufs=2))
         psum = ctx.enter_context(tc.psum_pool(name="psum", bufs=1))
 
-        offs_sb = keep.tile([P, E * C // 16], U16, name="offs_sb")
-        pos_sb = [keep.tile([P, T // 16], U16, name="pos_sb%d" % r) for r in range(3)]
+        offs_sb = keep.tile([P, SLOTS // PER_COLUMN], U16, name="offs_sb")
+        pos_sb = [keep.tile([P, T // PER_COLUMN], U16, name="pos_sb%d" % r) for r in range(TOP)]
         b_sb = keep.tile([P, E + 1], F32, name="b_sb")
-        gate_sb = keep.tile([P, 3, T], F32, name="gate_sb")
-        pairs = keep.tile([P, 2 * ((PLANES - 1) * T + WINDOW)], BF16, name="pairs", align_bytes=64)
-        words = pairs[:].bitcast(U32)
-        arena = keep.tile([P, 72 * UNIT], BF16, name="arena", align_bytes=64)
-        w16 = [keep.tile([P, E * WCOLS], BF16, name="w16_%d" % g, align_bytes=64) for g in range(PASSES)]
-        picked_at = [0, 12, 24, 36]
-        grouped_at = [24, 36, 48, 60]
+        gate_sb = keep.tile([P, TOP, T], F32, name="gate_sb")
+        planes = keep.tile([P, 2 * ((PLANES - 1) * T + WINDOW)], BF16, name="planes", align_bytes=64)
+        plane_words = planes[:].bitcast(U32)
+        rows16 = keep.tile([P, 2, T], BF16, name="rows16", align_bytes=64)
+        arena = keep.tile([P, ARENA_UNITS * UNIT], BF16, name="arena", align_bytes=64)
+        w16 = [keep.tile([P, E * W_COLS], BF16, name="w16_%d" % g, align_bytes=64) for g in range(PASSES)]
+        y = keep.tile([P, SLOTS], F32, name="y")
+        ys = keep.tile([P, T], F32, name="ys")
+        part = [keep.tile([P, T], F32, name="part%d" % r) for r in range(TOP)]
+        acc = [psum.tile([P, C], F32, name="acc%d" % e) for e in range(E)]
+        acc_shared = psum.tile([P, T], F32, name="acc_shared")
 
-        def units(a, count):
-            return arena[:, a * UNIT:(a + count) * UNIT]
+        def units(first, count):
+            return arena[:, first * UNIT:(first + count) * UNIT]
 
         x_raw = {}
         w_raw = {}
         for g in range(PASSES):
             for u in range(2):
-                if ("x", g, u) in LODGED:
-                    x_raw[g, u] = units(LODGED["x", g, u], 4).bitcast(F32).rearrange("p (e t) -> p e t", e=2)
+                if (g, u) in LODGED_X:
+                    x_raw[g, u] = units(LODGED_X[g, u], CHUNK_UNITS).bitcast(F32).rearrange("p (r t) -> p r t", r=2)
                 else:
                     x_raw[g, u] = keep.tile([P, 2, T], F32, name="x_raw%d_%d" % (g, u))[:]
             for c in range(CHUNKS):
-                if ("w", g, c) in LODGED:
-                    w_raw[g, c] = units(LODGED["w", g, c], 4).bitcast(F32).rearrange("p (e j n) -> p e j n", e=2, j=PACK)
+                if (g, c) in LODGED_W:
+                    raw = units(LODGED_W[g, c], CHUNK_UNITS).bitcast(F32)
+                    w_raw[g, c] = raw.rearrange("p (i j n) -> p i j n", i=2, j=PACK)
+                elif (g, c) in W_IN_X_TILE:
+                    w_raw[g, c] = x_raw[W_IN_X_TILE[g, c]].rearrange("p i (j n) -> p i j n", j=PACK)
                 else:
                     w_raw[g, c] = keep.tile([P, 2, PACK, N], F32, name="w_raw%d_%d" % (g, c))[:]
-            w_raw[g, SHARED] = keep.tile([P, 1, PACK, N], F32, name="w_raw%d_s" % g)[:]
+            w_raw[g, SHARED] = keep.tile([P, 1, PACK, N], F32, name="w_raw%d_shared" % g)[:]
 
-        y = keep.tile([P, E * C], F32, name="y")
-        ys = keep.tile([P, T], F32, name="ys")
-        warm = keep.tile([P, 8], F32, name="warm")
-        warm_out = keep.tile([P, 8], F32, name="warm_out")
-        acc = [psum.tile([P, C], F32, name="acc%d" % e) for e in range(E)]
-        acc_s = psum.tile([P, T], F32, name="acc_s")
-
-        def load_x(g, u):
-            rows = xT[g * K_PASS:(g + 1) * K_PASS, :].rearrange("(p u e) t -> p u e t", u=2, e=2)
-            nc.sync.dma_start(out=x_raw[g, u][:], in_=rows[:, u, :, :])
+        def x_rows(g, u):
+            return xT[g * K_PASS:(g + 1) * K_PASS, :].rearrange("(p u r) t -> p u r t", u=2, r=2)[:, u, :, :]
 
         def load_w(g, c):
-            e0 = 2 * c
-            e1 = min(e0 + 2, E + 1)
-            rows = w[e0:e1, g * K_PASS:(g + 1) * K_PASS, :].rearrange("e (p j) n -> p e (j n)", j=PACK)
-            nc.sync.dma_start(out=w_raw[g, c][:].rearrange("p e j n -> p e (j n)"), in_=rows)
+            experts = slice(2 * c, min(2 * c + 2, E + 1))
+            rows = w[experts, g * K_PASS:(g + 1) * K_PASS, :].rearrange("i (p j) n -> p i (j n)", j=PACK)
+            nc.sync.dma_start(out=w_raw[g, c].rearrange("p i j n -> p i (j n)"), in_=rows)
 
-        load_x(0, 1)
-        nc.sync.dma_start(offs_sb[:], offs)
-        for kind, g, i in LOADS:
-            if kind == "x":
-                load_x(g, i)
+        def plane(g, u):
+            first = 2 * PLANE_AT[g, u] * T
+            return planes[:, first:first + 2 * T].rearrange("p (t r) -> p t r", r=2)
+
+        def gpsimd_cast(dst, src):
+            nc.gpsimd.tensor_scalar(dst, src, 1.0, 0.0, MULT, ADD)
+
+        def cast_plane(g, u):
+            src = x_raw[g, u].rearrange("p r t -> p t r")
+            if (g, u) in GPSIMD_PLANES:
+                gpsimd_cast(plane(g, u), src)
             else:
-                load_w(g, i)
+                nc.scalar.copy(plane(g, u), src)
+
+        def scalar_cast_w(g, c, dst):
+            for i in range(w_raw[g, c].shape[1]):
+                cols = dst[:, i * W_COLS:(i + 1) * W_COLS].rearrange("p (m f j) -> p m j f", f=4, j=PACK)
+                nc.scalar.copy(cols, w_raw[g, c][:, i, :, :].rearrange("p j (m f) -> p m j f", f=4))
+
+        def cast_routed(g, c):
+            dst = w16[g][:, 2 * c * W_COLS:2 * (c + 1) * W_COLS]
+            if g < GPSIMD_PASSES:
+                gpsimd_cast(dst.rearrange("p (i n j) -> p i n j", n=N, j=PACK), w_raw[g, c].rearrange("p i j n -> p i n j"))
+            else:
+                scalar_cast_w(g, c, dst)
+
+        def gather_words(g, u, first_expert=0):
+            first = PLANE_AT[g, u] * T
+            window = plane_words[:, first:first + WINDOW]
+            dst = units(PICKED_AT[g] + u * HALF_UNITS, HALF_UNITS).bitcast(U32)[:, first_expert * C:]
+            nc.vector.tensor_copy(dst, window.indirect(offs_sb[:, first_expert * C // PER_COLUMN:]))
+
+        def gather_values(e):
+            dst = units(PICKED_AT[LAST], HALF_UNITS).rearrange("p (s r) -> p s r", r=2)
+            offsets = offs_sb[:, e * C // PER_COLUMN:(e + 1) * C // PER_COLUMN]
+            for r in range(2):
+                nc.scalar.activation(dst[:, e * C:(e + 1) * C, r], rows16[:, r, :].indirect(offsets), COPY)
+
+        def interleave(dst, words):
+            nc.scalar.copy(dst.bitcast(U32).rearrange("p (s u) -> p s u", u=2), words)
+
+        def picked_words(g):
+            return units(PICKED_AT[g], PASS_UNITS).bitcast(U32).rearrange("p (u s) -> p s u", u=2)
+
+        def grouped_chunk(g, c):
+            return units(GROUPED_AT[g] + c * CHUNK_UNITS, CHUNK_UNITS)
+
+        def interleave_tokens(g, dst):
+            lo, hi = PLANE_AT[g, 0], PLANE_AT[g, 1]
+            by_plane = plane_words[:, :PLANES * T].rearrange("p (i t) -> p t i", t=T)
+            interleave(dst, by_plane[:, :, lo:hi + 1:hi - lo])
+
+        def quantize(src, tag, bufs=2):
+            width = src.shape[1] // PACK
+            codes = ring.tile([P, width], U32, name=tag + "_codes", align_bytes=64, bufs=bufs)
+            scales = ring.tile([P, width], U8, name=tag + "_scales", align_bytes=64, bufs=bufs)
+            nc.vector.quantize_mx(out=codes[:].bitcast(FP8X4), scales=scales[:], in_=src)
+            return codes, scales
+
+        def multiply(dst, g, weights, w_cols, tokens, x_cols):
+            nc.tensor.matmul_mx(
+                out=dst, lhsT=weights[0][:, w_cols].bitcast(FP8X4), lhsT_scale=weights[1][:, w_cols],
+                rhs=tokens[0][:, x_cols].bitcast(FP8X4), rhs_scale=tokens[1][:, x_cols],
+                start=(g == 0), stop=(g == LAST))
+
+        def quantize_routed_weights(g):
+            four = quantize(w16[g][:, :4 * W_COLS], "w_four")
+            two = quantize(w16[g][:, 4 * W_COLS:], "w_two")
+            return [(four, e) for e in range(4)] + [(two, e) for e in range(2)]
+
+        def multiply_routed(g, weights):
+            for c in range(CHUNKS):
+                tokens = quantize(grouped_chunk(g, c), "x_slots", bufs=CHUNKS)
+                for i in range(2):
+                    e = 2 * c + i
+                    codes, place = weights[e]
+                    multiply(acc[e][:], g, codes, slice(place * N, (place + 1) * N), tokens, slice(i * C, (i + 1) * C))
+                    if g == LAST:
+                        nc.scalar.activation(y[:, e * C:(e + 1) * C], acc[e][:], GELU, bias=b_sb[:, e:e + 1])
+
+        def multiply_shared(g, tokens16, weights16):
+            weights = quantize(weights16, "w_shared")
+            tokens = quantize(tokens16, "x_tokens")
+            multiply(acc_shared[:], g, weights, slice(0, N), tokens, slice(0, T))
+
+        halves = [slice(0, T // 2), slice(T // 2, T)]
+        first_raw = x_raw[0, 1].rearrange("p r t -> p (r t)").rearrange("p (h r t) -> p h r t", h=2, r=2)
+        for h in range(2):
+            nc.sync.dma_start(out=first_raw[:, h, :, :], in_=x_rows(0, 1)[:, :, halves[h]])
+        nc.sync.dma_start(offs_sb[:], offs)
+        for g, u in [(0, 0), (1, 1), (LAST, 0)] + GPSIMD_PLANES:
+            nc.sync.dma_start(out=x_raw[g, u], in_=x_rows(g, u))
+        for g in range(LAST):
+            for c in range(CHUNKS + 1 if g < 2 else CHUNKS):
+                load_w(g, c)
+
+        zeros = planes[:, 2 * PLANES * T:]
+        nc.vector.memset(zeros[:, 2 * EDGE:3 * EDGE].bitcast(U32), 0)
+        nc.vector.memset(zeros[:, 3 * EDGE:].bitcast(U32), 0)
+        nc.scalar.activation(zeros[:, :EDGE], zeros[:, 2 * EDGE:3 * EDGE], GELU)
+        gpsimd_cast(zeros[:, EDGE:2 * EDGE], zeros[:, 2 * EDGE:3 * EDGE])
+
+        for h in range(2):
+            nc.vector.tensor_copy(plane(0, 1)[:, halves[h], :], first_raw[:, h, :, :].rearrange("p r t -> p t r"))
+        cast_plane(0, 0)
+        cast_plane(1, 1)
+        nc.scalar.copy(rows16[:], x_raw[LAST, 0])
+        for g, u in [(LAST, 0)] + GPSIMD_PLANES:
+            cast_plane(g, u)
+
+        for c in range(CHUNKS + 1):
+            load_w(LAST, c)
+        load_w(2, SHARED)
         nc.sync.dma_start(out=b_sb[:], in_=b)
         for r, pos in enumerate((pos1, pos2, pos3)):
             nc.sync.dma_start(pos_sb[r][:], pos)
         nc.sync.dma_start(out=gate_sb[:], in_=gate.rearrange("r n t -> n r t"))
 
-        nc.vector.memset(warm[:], 0.0)
-        nc.vector.memset(words[:, PLANES * T:], 0)
-        nc.scalar.activation(warm_out[:], warm[:], GELU)
-
-        def copy_on(engine, dst, src):
-            if engine == "vector":
-                nc.vector.tensor_copy(dst, src)
-            elif engine == "scalar":
-                nc.scalar.copy(dst, src)
-            else:
-                nc.gpsimd.tensor_scalar(dst, src, 1.0, 0.0, MULT, ADD)
-
-        def cast_pairs(g, u, engine):
-            s = 2 * PLANE_AT[g, u] * T
-            dst = pairs[:, s:s + 2 * T].rearrange("p (t e) -> p t e", e=2)
-            copy_on(engine, dst, x_raw[g, u][:].rearrange("p e t -> p t e"))
-
-        def gather(g, u):
-            s = PLANE_AT[g, u] * T
-            picked = units(picked_at[g], 12).bitcast(U32)
-            nc.vector.tensor_copy(picked[:, u * SLOTS:(u + 1) * SLOTS], words[:, s:s + WINDOW].indirect(offs_sb[:]))
-
-        def interleave(dst, src, engine):
-            copy_on(engine, dst.bitcast(U32).rearrange("p (s u) -> p s u", u=2), src)
-
-        def slot_tokens(g):
-            picked = units(picked_at[g], 12).bitcast(U32).rearrange("p (u s) -> p s u", u=2)
-            if g < LAST:
-                interleave(units(grouped_at[g], 12), picked, "scalar")
-            else:
-                for c in range(CHUNKS):
-                    interleave(units(grouped_at[g] + 4 * c, 4), picked[:, c * CHUNK:(c + 1) * CHUNK, :], "scalar")
-
-        def shared_tokens(g, dst, engine):
-            lo, hi = PLANE_AT[g, 0], PLANE_AT[g, 1]
-            planes = words[:, :PLANES * T].rearrange("p (i t) -> p t i", t=T)
-            interleave(dst, planes[:, :, lo:hi + 1:hi - lo], engine)
-
-        def cast_w(key, dst, engine):
-            if engine == "gpsimd":
-                copy_on(engine, dst.rearrange("p (e n j) -> p e n j", n=N, j=PACK), w_raw[key][:].rearrange("p e j n -> p e n j"))
-            else:
-                for e in range(w_raw[key].shape[1]):
-                    cols = dst[:, e * WCOLS:(e + 1) * WCOLS]
-                    copy_on(engine, cols.rearrange("p (m i j) -> p m j i", i=4, j=PACK),
-                            w_raw[key][:, e, :, :].rearrange("p j (m i) -> p m j i", i=4))
-
-        def cast_routed(g, c):
-            cast_w((g, c), w16[g][:, 2 * c * WCOLS:2 * (c + 1) * WCOLS], W_ENGINE.get((g, c), "scalar"))
-
-        def cast_shared(g, at):
-            cast_w((g, SHARED), units(at + 4, 1), "scalar")
-            shared_tokens(g, units(at, 4), "scalar")
-
-        def quantize(src, tag):
-            width = src.shape[1] // PACK
-            codes = ring.tile([P, width], U32, name=tag + "_codes", align_bytes=64)
-            scales = ring.tile([P, width], U8, name=tag + "_scales", align_bytes=64)
-            nc.vector.quantize_mx(out=codes[:].bitcast(FP8X4), scales=scales[:], in_=src)
-            return codes, scales
-
-        wq = {}
-
-        def multiply(dst, place, wcodes, w0, xcodes, x_cols):
-            w_cols = slice(w0, w0 + N)
-            nc.tensor.matmul_mx(
-                out=dst, lhsT=wcodes[0][:, w_cols].bitcast(FP8X4), lhsT_scale=wcodes[1][:, w_cols],
-                rhs=xcodes[0][:, x_cols].bitcast(FP8X4), rhs_scale=xcodes[1][:, x_cols],
-                start=(place == 0), stop=(place == LAST))
-
-        def routed_tokens(g):
-            for c in (range(CHUNKS) if g == LAST else reversed(range(CHUNKS))):
-                xq = quantize(units(grouped_at[g] + 4 * c, 4), "x")
-                for i in range(2):
-                    e = 2 * c + i
-                    codes, first = (wq[g][0], e) if c < 2 else (wq[g][1], i)
-                    multiply(acc[e][:], g, codes, first * N, xq, slice(i * C, (i + 1) * C))
-                    if g == LAST:
-                        nc.scalar.activation(y[:, e * C:(e + 1) * C], acc[e][:], GELU, bias=b_sb[:, e:e + 1])
-
-        def routed_weights(g):
-            wq[g] = (quantize(w16[g][:, :4 * WCOLS], "w"), quantize(w16[g][:, 4 * WCOLS:], "wr"))
-
-        def shared_pass(place, tokens, weights):
-            ws = quantize(weights, "ws")
-            xs = quantize(tokens, "xs")
-            multiply(acc_s[:], place, ws, 0, xs, slice(0, T))
-
-        part = [keep.tile([P, T], F32, name="part%d" % r) for r in range(3)]
-
-        def fetch(r):
-            nc.vector.tensor_tensor(part[r][:], y[:].indirect(pos_sb[r][:]), gate_sb[:, r, :], MULT)
-
-        def both_gathers(g):
-            gather(g, 1)
-            gather(g, 0)
-
-        def batch(g):
-            routed_weights(g)
-            shared_pass(g, units(picked_at[g], 4), units(picked_at[g] + 4, 1))
-            routed_tokens(g)
-
-        cast_pairs(0, 1, "vector")
-        for g, u in ((0, 0), (1, 1), (1, 0), (2, 1)):
-            cast_pairs(g, u, "scalar")
-        cast_routed(0, 0)
-        cast_routed(0, 1)
-        both_gathers(0)
-        slot_tokens(0)
-        cast_routed(0, 2)
-        cast_shared(0, picked_at[0])
-        cast_pairs(2, 0, "scalar")
-        both_gathers(1)
-        slot_tokens(1)
-        batch(0)
-        cast_pairs(3, 1, "scalar")
-        for c in range(CHUNKS):
-            cast_routed(1, c)
-        cast_shared(1, picked_at[1])
-        cast_pairs(3, 0, "scalar")
-        both_gathers(2)
-        batch(1)
-        slot_tokens(2)
-        for g in (2, 3):
+        early_tokens = [units(at, CHUNK_UNITS) for at in EARLY_TOKENS_AT]
+        early_weights = [units(at + CHUNK_UNITS, 1) for at in EARLY_TOKENS_AT]
+        for g in range(GPSIMD_PASSES):
             for c in range(CHUNKS):
                 cast_routed(g, c)
-        weights2 = units(picked_at[2] + 5, 1)
-        cast_w((2, SHARED), weights2, "scalar")
-        cast_shared(3, picked_at[2])
-        both_gathers(3)
-        routed_weights(2)
-        routed_tokens(2)
-        slot_tokens(3)
-        routed_weights(3)
-        shared_pass(2, units(picked_at[2], 4), units(picked_at[2] + 4, 1))
-        routed_tokens(3)
-        tokens2 = units(grouped_at[LAST] + 8, 4)
-        shared_tokens(2, tokens2, "vector")
-        shared_pass(3, tokens2, weights2)
-        nc.scalar.activation(ys[:], acc_s[:], GELU, bias=b_sb[:, E:E + 1])
-        for r in range(3):
-            fetch(r)
-        halves = [slice(0, T // 2), slice(T // 2, T)]
+        for e in range(SCALAR_EXPERTS):
+            gather_values(e)
+        for g in range(2):
+            gather_words(g, 1)
+            gather_words(g, 0)
+            interleave(units(GROUPED_AT[g], PASS_UNITS), picked_words(g))
+            scalar_cast_w(g, SHARED, early_weights[g])
+            interleave_tokens(g, early_tokens[g])
+        gather_words(2, 1)
+        gather_words(2, 0)
+        cast_routed(2, 0)
+        cast_routed(2, 1)
+        interleave(units(GROUPED_AT[2], PASS_UNITS), picked_words(2))
+        gather_words(LAST, 1)
+        gather_words(LAST, 0, SCALAR_EXPERTS)
+        cast_routed(2, 2)
+
+        for g in range(2):
+            weights = quantize_routed_weights(g)
+            multiply_shared(g, early_tokens[g], early_weights[g])
+            multiply_routed(g, weights)
+        multiply_routed(2, quantize_routed_weights(2))
+        for c in range(CHUNKS):
+            cast_routed(LAST, c)
+        late_weights = {g: units(LATE_WEIGHTS_AT + g - 2, 1) for g in (2, LAST)}
+        for g in (2, LAST):
+            scalar_cast_w(g, SHARED, late_weights[g])
+        for c in range(CHUNKS):
+            interleave(grouped_chunk(LAST, c), picked_words(LAST)[:, c * CHUNK:(c + 1) * CHUNK, :])
+        late_tokens = {g: units(PICKED_AT[LAST] + (g - 2) * HALF_UNITS, CHUNK_UNITS) for g in (2, LAST)}
+        for g in (2, LAST):
+            interleave_tokens(g, late_tokens[g])
+        multiply_routed(LAST, quantize_routed_weights(LAST))
+        for g in (2, LAST):
+            multiply_shared(g, late_tokens[g], late_weights[g])
+        nc.scalar.activation(ys[:], acc_shared[:], GELU, bias=b_sb[:, E:E + 1])
+
+        for r in range(TOP):
+            nc.vector.tensor_tensor(part[r][:], y[:].indirect(pos_sb[r][:]), gate_sb[:, r, :], MULT)
         nc.vector.tensor_tensor(part[0][:], part[0][:], part[1][:], ADD)
-        for h in halves:
-            nc.vector.tensor_tensor(part[2][:, h], part[2][:, h], ys[:, h], ADD)
-        for h in halves:
-            nc.vector.tensor_tensor(part[1][:, h], part[0][:, h], part[2][:, h], ADD)
-            nc.sync.dma_start(out=out[:, h], in_=part[1][:, h])
+        for half in halves:
+            nc.vector.tensor_tensor(part[2][:, half], part[2][:, half], ys[:, half], ADD)
+        for half in halves:
+            nc.vector.tensor_tensor(part[1][:, half], part[0][:, half], part[2][:, half], ADD)
+            nc.sync.dma_start(out=out[:, half], in_=part[1][:, half])

from contextlib import ExitStack

import concourse.mybir as mybir

K, T, E, C, N = 2048, 512, 6, 256, 128
FLOPS = 2 * K * N * (E * C + T)

F32 = mybir.dt.float32
BF16 = mybir.dt.bfloat16
U32 = mybir.dt.uint32
U16 = mybir.dt.uint16
U8 = mybir.dt.uint8
FP8X4 = mybir.dt.float8_e4m3fn_x4
GELU = mybir.ActivationFunctionType.Gelu_apprx_tanh
COPY = mybir.ActivationFunctionType.Copy
MULT = mybir.AluOpType.mult
ADD = mybir.AluOpType.add

P = 128
PACK = 4
K_PASS = P * PACK
PASSES = K // K_PASS
LAST = PASSES - 1
TOP = 3
SLOTS = E * C
PER_COLUMN = 16
CHUNK = 2 * C
CHUNKS = SLOTS // CHUNK
SHARED = CHUNKS
W_COLS = N * PACK

WINDOW = 4 * T
PLANES = 2 * PASSES
PLANE_AT = {(3, 0): 0, (2, 0): 1, (3, 1): 2, (1, 0): 3, (2, 1): 4, (0, 0): 5, (1, 1): 6, (0, 1): 7}
EDGE = 16

UNIT = 512
HALF_UNITS = 6
PASS_UNITS = 12
CHUNK_UNITS = 4
PICKED_AT = [PASS_UNITS * g for g in range(PASSES)]
GROUPED_AT = [PASS_UNITS * PASSES] + PICKED_AT[:LAST]
EARLY_TOKENS_AT = [60, 65]
LATE_WEIGHTS_AT = 70
ARENA_UNITS = 74

LODGED_X = {(3, 1): GROUPED_AT[0], (1, 1): PICKED_AT[2], (1, 0): PICKED_AT[2] + 4, (2, 1): PICKED_AT[2] + 8,
            (2, 0): LATE_WEIGHTS_AT}
LODGED_W = {(0, 0): EARLY_TOKENS_AT[1] - 2}
W_IN_X_TILE = {(LAST, 0): (0, 1), (LAST, 1): (0, 0), (LAST, 2): (LAST, 0)}

SCALAR_EXPERTS = 4
GPSIMD_PLANES = [(1, 0), (2, 1), (2, 0), (3, 1)]
GPSIMD_PASSES = 2


def tile_moe_shr_lin_gelu_kernel(tc, xT, w, b, gate, offs, pos1, pos2, pos3, out):
    nc = tc.nc
    with ExitStack() as ctx:
        keep = ctx.enter_context(tc.tile_pool(name="keep", bufs=1))
        ring = ctx.enter_context(tc.tile_pool(name="ring", bufs=2))
        psum = ctx.enter_context(tc.psum_pool(name="psum", bufs=1))

        offs_sb = keep.tile([P, SLOTS // PER_COLUMN], U16, name="offs_sb")
        pos_sb = [keep.tile([P, T // PER_COLUMN], U16, name="pos_sb%d" % r) for r in range(TOP)]
        b_sb = keep.tile([P, E + 1], F32, name="b_sb")
        gate_sb = keep.tile([P, TOP, T], F32, name="gate_sb")
        planes = keep.tile([P, 2 * ((PLANES - 1) * T + WINDOW)], BF16, name="planes", align_bytes=64)
        plane_words = planes[:].bitcast(U32)
        rows16 = keep.tile([P, 2, T], BF16, name="rows16", align_bytes=64)
        arena = keep.tile([P, ARENA_UNITS * UNIT], BF16, name="arena", align_bytes=64)
        w16 = [keep.tile([P, E * W_COLS], BF16, name="w16_%d" % g, align_bytes=64) for g in range(PASSES)]
        y = keep.tile([P, SLOTS], F32, name="y")
        ys = keep.tile([P, T], F32, name="ys")
        part = [keep.tile([P, T], F32, name="part%d" % r) for r in range(TOP)]
        acc = [psum.tile([P, C], F32, name="acc%d" % e) for e in range(E)]
        acc_shared = psum.tile([P, T], F32, name="acc_shared")

        def units(first, count):
            return arena[:, first * UNIT:(first + count) * UNIT]

        x_raw = {}
        w_raw = {}
        for g in range(PASSES):
            for u in range(2):
                if (g, u) in LODGED_X:
                    x_raw[g, u] = units(LODGED_X[g, u], CHUNK_UNITS).bitcast(F32).rearrange("p (r t) -> p r t", r=2)
                else:
                    x_raw[g, u] = keep.tile([P, 2, T], F32, name="x_raw%d_%d" % (g, u))[:]
            for c in range(CHUNKS):
                if (g, c) in LODGED_W:
                    raw = units(LODGED_W[g, c], CHUNK_UNITS).bitcast(F32)
                    w_raw[g, c] = raw.rearrange("p (i j n) -> p i j n", i=2, j=PACK)
                elif (g, c) in W_IN_X_TILE:
                    w_raw[g, c] = x_raw[W_IN_X_TILE[g, c]].rearrange("p i (j n) -> p i j n", j=PACK)
                else:
                    w_raw[g, c] = keep.tile([P, 2, PACK, N], F32, name="w_raw%d_%d" % (g, c))[:]
            w_raw[g, SHARED] = keep.tile([P, 1, PACK, N], F32, name="w_raw%d_shared" % g)[:]

        def x_rows(g, u):
            return xT[g * K_PASS:(g + 1) * K_PASS, :].rearrange("(p u r) t -> p u r t", u=2, r=2)[:, u, :, :]

        def load_w(g, c):
            experts = slice(2 * c, min(2 * c + 2, E + 1))
            rows = w[experts, g * K_PASS:(g + 1) * K_PASS, :].rearrange("i (p j) n -> p i (j n)", j=PACK)
            nc.sync.dma_start(out=w_raw[g, c].rearrange("p i j n -> p i (j n)"), in_=rows)

        def plane(g, u):
            first = 2 * PLANE_AT[g, u] * T
            return planes[:, first:first + 2 * T].rearrange("p (t r) -> p t r", r=2)

        def gpsimd_cast(dst, src):
            nc.gpsimd.tensor_scalar(dst, src, 1.0, 0.0, MULT, ADD)

        def cast_plane(g, u):
            src = x_raw[g, u].rearrange("p r t -> p t r")
            if (g, u) in GPSIMD_PLANES:
                gpsimd_cast(plane(g, u), src)
            else:
                nc.scalar.copy(plane(g, u), src)

        def scalar_cast_w(g, c, dst):
            for i in range(w_raw[g, c].shape[1]):
                cols = dst[:, i * W_COLS:(i + 1) * W_COLS].rearrange("p (m f j) -> p m j f", f=4, j=PACK)
                nc.scalar.copy(cols, w_raw[g, c][:, i, :, :].rearrange("p j (m f) -> p m j f", f=4))

        def cast_routed(g, c):
            dst = w16[g][:, 2 * c * W_COLS:2 * (c + 1) * W_COLS]
            if g < GPSIMD_PASSES:
                gpsimd_cast(dst.rearrange("p (i n j) -> p i n j", n=N, j=PACK), w_raw[g, c].rearrange("p i j n -> p i n j"))
            else:
                scalar_cast_w(g, c, dst)

        def gather_words(g, u, first_expert=0):
            first = PLANE_AT[g, u] * T
            window = plane_words[:, first:first + WINDOW]
            dst = units(PICKED_AT[g] + u * HALF_UNITS, HALF_UNITS).bitcast(U32)[:, first_expert * C:]
            nc.vector.tensor_copy(dst, window.indirect(offs_sb[:, first_expert * C // PER_COLUMN:]))

        def gather_values(e):
            dst = units(PICKED_AT[LAST], HALF_UNITS).rearrange("p (s r) -> p s r", r=2)
            offsets = offs_sb[:, e * C // PER_COLUMN:(e + 1) * C // PER_COLUMN]
            for r in range(2):
                nc.scalar.activation(dst[:, e * C:(e + 1) * C, r], rows16[:, r, :].indirect(offsets), COPY)

        def interleave(dst, words):
            nc.scalar.copy(dst.bitcast(U32).rearrange("p (s u) -> p s u", u=2), words)

        def picked_words(g):
            return units(PICKED_AT[g], PASS_UNITS).bitcast(U32).rearrange("p (u s) -> p s u", u=2)

        def grouped_chunk(g, c):
            return units(GROUPED_AT[g] + c * CHUNK_UNITS, CHUNK_UNITS)

        def interleave_tokens(g, dst):
            lo, hi = PLANE_AT[g, 0], PLANE_AT[g, 1]
            by_plane = plane_words[:, :PLANES * T].rearrange("p (i t) -> p t i", t=T)
            interleave(dst, by_plane[:, :, lo:hi + 1:hi - lo])

        def quantize(src, tag, bufs=2):
            width = src.shape[1] // PACK
            codes = ring.tile([P, width], U32, name=tag + "_codes", align_bytes=64, bufs=bufs)
            scales = ring.tile([P, width], U8, name=tag + "_scales", align_bytes=64, bufs=bufs)
            nc.vector.quantize_mx(out=codes[:].bitcast(FP8X4), scales=scales[:], in_=src)
            return codes, scales

        def multiply(dst, g, weights, w_cols, tokens, x_cols):
            nc.tensor.matmul_mx(
                out=dst, lhsT=weights[0][:, w_cols].bitcast(FP8X4), lhsT_scale=weights[1][:, w_cols],
                rhs=tokens[0][:, x_cols].bitcast(FP8X4), rhs_scale=tokens[1][:, x_cols],
                start=(g == 0), stop=(g == LAST))

        def quantize_routed_weights(g):
            four = quantize(w16[g][:, :4 * W_COLS], "w_four")
            two = quantize(w16[g][:, 4 * W_COLS:], "w_two")
            return [(four, e) for e in range(4)] + [(two, e) for e in range(2)]

        def multiply_routed(g, weights):
            for c in range(CHUNKS):
                tokens = quantize(grouped_chunk(g, c), "x_slots", bufs=CHUNKS)
                for i in range(2):
                    e = 2 * c + i
                    codes, place = weights[e]
                    multiply(acc[e][:], g, codes, slice(place * N, (place + 1) * N), tokens, slice(i * C, (i + 1) * C))
                    if g == LAST:
                        nc.scalar.activation(y[:, e * C:(e + 1) * C], acc[e][:], GELU, bias=b_sb[:, e:e + 1])

        def multiply_shared(g, tokens16, weights16):
            weights = quantize(weights16, "w_shared")
            tokens = quantize(tokens16, "x_tokens")
            multiply(acc_shared[:], g, weights, slice(0, N), tokens, slice(0, T))

        halves = [slice(0, T // 2), slice(T // 2, T)]
        first_raw = x_raw[0, 1].rearrange("p r t -> p (r t)").rearrange("p (h r t) -> p h r t", h=2, r=2)
        for h in range(2):
            nc.sync.dma_start(out=first_raw[:, h, :, :], in_=x_rows(0, 1)[:, :, halves[h]])
        nc.sync.dma_start(offs_sb[:], offs)
        for g, u in [(0, 0), (1, 1), (LAST, 0)] + GPSIMD_PLANES:
            nc.sync.dma_start(out=x_raw[g, u], in_=x_rows(g, u))
        for g in range(LAST):
            for c in range(CHUNKS + 1 if g < 2 else CHUNKS):
                load_w(g, c)

        zeros = planes[:, 2 * PLANES * T:]
        nc.vector.memset(zeros[:, 2 * EDGE:3 * EDGE].bitcast(U32), 0)
        nc.vector.memset(zeros[:, 3 * EDGE:].bitcast(U32), 0)
        nc.scalar.activation(zeros[:, :EDGE], zeros[:, 2 * EDGE:3 * EDGE], GELU)
        gpsimd_cast(zeros[:, EDGE:2 * EDGE], zeros[:, 2 * EDGE:3 * EDGE])

        for h in range(2):
            nc.vector.tensor_copy(plane(0, 1)[:, halves[h], :], first_raw[:, h, :, :].rearrange("p r t -> p t r"))
        cast_plane(0, 0)
        cast_plane(1, 1)
        nc.scalar.copy(rows16[:], x_raw[LAST, 0])
        for g, u in [(LAST, 0)] + GPSIMD_PLANES:
            cast_plane(g, u)

        for c in range(CHUNKS + 1):
            load_w(LAST, c)
        load_w(2, SHARED)
        nc.sync.dma_start(out=b_sb[:], in_=b)
        for r, pos in enumerate((pos1, pos2, pos3)):
            nc.sync.dma_start(pos_sb[r][:], pos)
        nc.sync.dma_start(out=gate_sb[:], in_=gate.rearrange("r n t -> n r t"))

        early_tokens = [units(at, CHUNK_UNITS) for at in EARLY_TOKENS_AT]
        early_weights = [units(at + CHUNK_UNITS, 1) for at in EARLY_TOKENS_AT]
        for g in range(GPSIMD_PASSES):
            for c in range(CHUNKS):
                cast_routed(g, c)
        for e in range(SCALAR_EXPERTS):
            gather_values(e)
        for g in range(2):
            gather_words(g, 1)
            gather_words(g, 0)
            interleave(units(GROUPED_AT[g], PASS_UNITS), picked_words(g))
            scalar_cast_w(g, SHARED, early_weights[g])
            interleave_tokens(g, early_tokens[g])
        gather_words(2, 1)
        gather_words(2, 0)
        cast_routed(2, 0)
        cast_routed(2, 1)
        interleave(units(GROUPED_AT[2], PASS_UNITS), picked_words(2))
        gather_words(LAST, 1)
        gather_words(LAST, 0, SCALAR_EXPERTS)
        cast_routed(2, 2)

        for g in range(2):
            weights = quantize_routed_weights(g)
            multiply_shared(g, early_tokens[g], early_weights[g])
            multiply_routed(g, weights)
        multiply_routed(2, quantize_routed_weights(2))
        for c in range(CHUNKS):
            cast_routed(LAST, c)
        late_weights = {g: units(LATE_WEIGHTS_AT + g - 2, 1) for g in (2, LAST)}
        for g in (2, LAST):
            scalar_cast_w(g, SHARED, late_weights[g])
        for c in range(CHUNKS):
            interleave(grouped_chunk(LAST, c), picked_words(LAST)[:, c * CHUNK:(c + 1) * CHUNK, :])
        late_tokens = {g: units(PICKED_AT[LAST] + (g - 2) * HALF_UNITS, CHUNK_UNITS) for g in (2, LAST)}
        for g in (2, LAST):
            interleave_tokens(g, late_tokens[g])
        multiply_routed(LAST, quantize_routed_weights(LAST))
        for g in (2, LAST):
            multiply_shared(g, late_tokens[g], late_weights[g])
        nc.scalar.activation(ys[:], acc_shared[:], GELU, bias=b_sb[:, E:E + 1])

        for r in range(TOP):
            nc.vector.tensor_tensor(part[r][:], y[:].indirect(pos_sb[r][:]), gate_sb[:, r, :], MULT)
        nc.vector.tensor_tensor(part[0][:], part[0][:], part[1][:], ADD)
        for half in halves:
            nc.vector.tensor_tensor(part[2][:, half], part[2][:, half], ys[:, half], ADD)
        for half in halves:
            nc.vector.tensor_tensor(part[1][:, half], part[0][:, half], part[2][:, half], ADD)
            nc.sync.dma_start(out=out[:, half], in_=part[1][:, half])
